import numpy as np
import ml_dtypes


def mxq(x, axis, fmt="e4m3"):
    dtype, down = {"e4m3": (ml_dtypes.float8_e4m3fn, 7), "e5m2": (ml_dtypes.float8_e5m2, 14)}[fmt]
    v = np.moveaxis(np.asarray(x, np.float32).astype(ml_dtypes.bfloat16).astype(np.float64), axis, -1)
    blocks = v.reshape(v.shape[:-1] + (-1, 32))
    amax = np.abs(blocks).max(-1, keepdims=True)
    byte = np.maximum(np.where(amax > 0, np.frexp(amax)[1] - 1 + 127, 0) - down, 1)
    scale = np.exp2(byte - 127.0)
    codes = (blocks / scale).astype(np.float32).astype(dtype).astype(np.float64)
    return np.moveaxis((codes * scale).reshape(v.shape), -1, axis)


WIDE = False


def mx_kscale(k):
    if not WIDE:
        return np.ones(k)
    levels = np.array([10, -10, 5, -5, 0])
    if k % 512:
        return np.exp2(np.random.permutation(np.resize(levels, k // 32))).repeat(32)
    a = np.empty((k // 512, 16))
    for p in range(k // 512):
        a[p, :8] = np.random.permutation(np.resize(levels, 8))
        for g in range(8):
            far = levels[np.abs(levels - a[p, g]) >= 10]
            a[p, g + 8] = far[np.random.randint(len(far))]
    return np.exp2(a.ravel()).repeat(32)


def f64(x):
    return np.asarray(x).astype(np.float64)


def striped(idx):
    return np.tile(idx.reshape(-1, 16).T, (8, 1)).astype(np.uint16)


def unstriped(offs):
    return offs[:16].T.reshape(-1).astype(np.int64)


def d_silu(v):
    s = 1.0 / (1.0 + np.exp(-np.maximum(v, -700.0)))
    return s * (1.0 + v * (1.0 - s))


K, T, E, C, H, N = 512, 1536, 3, 512, 512, 512


def by_expert(wq, xq):
    return np.concatenate([wq[e].T @ xq[:, e * C:(e + 1) * C] for e in range(E)], axis=1)


def setup_inputs():
    n = np.random.standard_normal
    slot_token = np.random.permutation(T)[:E * C]
    s = mx_kscale(N)[:, None]
    z = np.ones(T); z[slot_token] = mx_kscale(E * C)
    return {
        "xT": (n((K, T)) * z[None, :]).astype(np.float32),
        "dyT": (n((N, T)) * s).astype(np.float32),
        "a": n((H, E * C)).astype(np.float32),
        "w2": (n((E, N, H)) / np.sqrt(N) / s[None]).astype(np.float32),
        "gate": np.tile(np.random.uniform(0.2, 1.0, E * C) / z[slot_token], (N, 1)).astype(np.float32),
        "offs": striped(slot_token),
    }


def reference(xT, dyT, a, w2, gate, offs):
    idx = unstriped(offs)
    gq = mxq(f64(gate) * f64(dyT)[:, idx], 0, "e4m3")
    dh = by_expert(mxq(f64(w2), 1, "e4m3"), gq)
    da = mxq(dh * d_silu(f64(a)), 1, "e4m3")
    xq = mxq(f64(xT)[:, idx], 1, "e4m3")
    return np.stack([(xq[:, e * C:(e + 1) * C] @ da[:, e * C:(e + 1) * C].T) for e in range(E)])

@@ -1,0 +1,249 @@
+from contextlib import ExitStack
+
+import concourse.mybir as mybir
+from concourse.masks import make_identity
+
+K, T, E, C, H, N = 512, 1536, 3, 512, 512, 512
+FLOPS = 2 * E * C * (N * H + K * H)
+BYTES = 4 * (K * T + N * T + H * E * C + E * N * H + E * C + E * K * H) + 2 * 128 * 96
+
+F32 = mybir.dt.float32
+BF16 = mybir.dt.bfloat16
+U32 = mybir.dt.uint32
+U16 = mybir.dt.uint16
+U8 = mybir.dt.uint8
+FP8X4 = mybir.dt.float8_e4m3fn_x4
+ALU = mybir.AluOpType
+ACT = mybir.ActivationFunctionType
+
+P = 128
+PACK = 4
+BLOCKS = 4
+OFFS_COLS = C // 16
+
+
+def tile_moe_mlp_silu_kernel(tc, xT, dyT, a, w2, gate, offs, out):
+    nc = tc.nc
+    with ExitStack() as ctx:
+        keep = ctx.enter_context(tc.tile_pool(name="keep", bufs=1))
+        ring = ctx.enter_context(tc.tile_pool(name="ring", bufs=2))
+        psum = ctx.enter_context(tc.psum_pool(name="psum", bufs=2))
+
+        offsets = keep.tile([P, E * OFFS_COLS], U16, name="offsets")
+        nc.sync.dma_start(offsets[:], offs)
+
+        dy_rows = dyT.rearrange("(p j) t -> p j t", j=PACK)
+        dy_sb = [keep.tile([P, T], F32, name=f"dy{j}") for j in range(PACK)]
+        x_sb = [keep.tile([P, T], F32, name=f"x{b}") for b in range(BLOCKS)]
+        a_sb = [[keep.tile([P, 2, C], F32, name=f"a{e}_{h}") for h in range(2)] for e in range(E)]
+        gate_sb = [keep.tile([P, C], F32, name=f"gate{e}") for e in range(E)]
+        w_sb = [keep.tile([P, PACK, H], F32, name=f"w{e}") for e in range(E)]
+
+        def load_a(e):
+            for h in range(2):
+                rows = a[h * 2 * P:(h + 1) * 2 * P, e * C:(e + 1) * C]
+                nc.sync.dma_start(a_sb[e][h][:], rows.rearrange("(b p) s -> p b s", p=P))
+
+        def load_w(e):
+            nc.sync.dma_start(w_sb[e][:], w2[e].rearrange("(p j) i -> p j i", j=PACK))
+
+        def load_gate(e):
+            nc.sync.dma_start(gate_sb[e][:], gate[0:P, e * C:(e + 1) * C])
+
+        def load_dy(j):
+            nc.sync.dma_start(dy_sb[j][:], dy_rows[:, j, :])
+
+        def load_x(b):
+            nc.sync.dma_start(x_sb[b][:], xT[b * P:(b + 1) * P, :])
+
+        load_a(0)
+        load_dy(0)
+        load_dy(1)
+        load_a(1)
+        load_dy(2)
+        load_dy(3)
+        load_gate(0)
+        load_w(0)
+        load_gate(1)
+        load_x(0)
+        load_x(1)
+        load_w(1)
+        load_x(2)
+        load_x(3)
+        load_w(2)
+        load_a(2)
+        load_gate(2)
+
+        ident = keep.tile([P, P], F32, name="ident")
+        make_identity(nc, ident[:])
+
+        work = [keep.tile([P, PACK * C], F32, name=f"work{n}") for n in range(3)]
+        sig_in = [work[0], work[2], work[2]]
+        dy_in = [work[1][:], work[0][:], w_sb[1][:].rearrange("p j i -> p (j i)")]
+        rows_bf = [[keep.tile([P, C], BF16, name=f"rows{n}_{b}") for b in range(BLOCKS)] for n in range(3)]
+        da_in = [rows_bf[2], rows_bf[2], rows_bf[0]]
+        x_in = [rows_bf[0], rows_bf[1], rows_bf[2]]
+
+        banks = [psum.tile([P, C], F32, name=f"bank{n}", bufs=1) for n in range(8)]
+        dh_banks = [(0, 1, 2, 3), (2, 3, 4, 5), (4, 5, 6, 7)]
+        da_banks = [(6, 7), (6, 7), (5, 6)]
+        x_banks = [(4, 0), (5, 1), (4, 7)]
+        out_banks = [(0, 1, 2, 3), (0, 1, 2, 3), (0, 1, 2, 3)]
+
+        def gather(on_vector, dst, window, e):
+            picked = window[:].indirect(offsets[:, e * OFFS_COLS:(e + 1) * OFFS_COLS])
+            if on_vector:
+                nc.vector.tensor_copy(dst, picked)
+            else:
+                nc.scalar.activation(dst, picked, ACT.Copy)
+
+        def quantise(values, name, bufs):
+            width = values.shape[1] // PACK
+            codes = ring.tile([P, width], U32, name=name + "_codes", align_bytes=64, bufs=bufs)
+            scales = ring.tile([P, width], U8, name=name + "_scales", align_bytes=64, bufs=bufs)
+            nc.vector.quantize_mx(out=codes[:].bitcast(FP8X4), scales=scales[:], in_=values)
+            return codes, scales
+
+        def psum_copy(on_vector, dst, src):
+            if on_vector:
+                nc.vector.tensor_copy(dst, src)
+            else:
+                nc.scalar.copy(dst, src)
+
+        def turn(pair, dst, on_vector, n):
+            bank = banks[n][:].rearrange("p (b u c) -> p b u c", b=2, u=2)
+            for b in range(2):
+                words = pair[b][:].bitcast(F32)
+                for u in range(2):
+                    nc.tensor.transpose(bank[:, b, u, :], words[:, u::2], ident[:])
+            psum_copy(on_vector, dst.bitcast(F32).rearrange("p (b c u) -> p b c u", b=2, u=2),
+                      bank.rearrange("p b u c -> p b c u"))
+
+        def sigmoid(e):
+            for h in range(2):
+                nc.scalar.activation(sig_in[e][:, h * 2 * C:(h + 1) * 2 * C],
+                                     a_sb[e][h][:].rearrange("p b s -> p (b s)"), ACT.Sigmoid)
+
+        def silu_slope(e):
+            for step in range(2):
+                for h in range(2):
+                    v = a_sb[e][h][:].rearrange("p b s -> p (b s)")
+                    sig = sig_in[e][:, h * 2 * C:(h + 1) * 2 * C]
+                    if step == 0:
+                        nc.vector.scalar_tensor_tensor(v, sig, 1.0, v, ALU.subtract, ALU.mult)
+                    else:
+                        nc.vector.scalar_tensor_tensor(v, v, 1.0, sig, ALU.subtract, ALU.mult)
+
+        g_mx, w_mx, da_mx, x_mx, g_bf, w_bf, da_turned, x_turned = {}, {}, {}, {}, {}, {}, {}, {}
+
+        def gather_dy(e):
+            for j in range(PACK):
+                gather((j, e) in ((0, 1),), dy_in[e][:, j * C:(j + 1) * C], dy_sb[j], e)
+
+        def gate_rows(e):
+            g_bf[e] = ring.tile([P, C * PACK], BF16, name="g_bf", align_bytes=64)
+            gate_e = gate_sb[e][:].rearrange("p (c i) -> p c i", i=2)
+            nc.vector.tensor_tensor(g_bf[e][:].rearrange("p (c i j) -> p c j i", i=2, j=PACK),
+                                    dy_in[e][:].rearrange("p (j c i) -> p c j i", j=PACK, i=2),
+                                    gate_e.unsqueeze(2).to_broadcast([P, C // 2, PACK, 2]), ALU.mult)
+
+        def cast_w(e):
+            w_bf[e] = ring.tile([P, H * PACK], BF16, name="w_bf", align_bytes=64)
+            nc.vector.tensor_copy(w_bf[e][:].rearrange("p (c i j) -> p c j i", i=2, j=PACK),
+                                  w_sb[e][:].rearrange("p j (c i) -> p c j i", i=2))
+
+        def quantise_g(e):
+            g_mx[e] = quantise(g_bf[e][:], "g", 2)
+
+        def quantise_w(e):
+            w_mx[e] = quantise(w_bf[e][:], "w", 3)
+
+        def hidden_gradient(e):
+            da_turned[e] = ring.tile([P, H * PACK], BF16, name="da_turned", align_bytes=64)
+            for h in range(2):
+                for b in range(2 * h, 2 * h + 2):
+                    dh = banks[dh_banks[e][b]]
+                    cols = slice(b * P, (b + 1) * P)
+                    nc.tensor.matmul_mx(out=dh[:], lhsT=w_mx[e][0][:, cols].bitcast(FP8X4), lhsT_scale=w_mx[e][1][:, cols],
+                                        rhs=g_mx[e][0][:].bitcast(FP8X4), rhs_scale=g_mx[e][1][:], start=True, stop=True)
+                    nc.vector.scalar_tensor_tensor(da_in[e][b][:], a_sb[e][h][:, b % 2, :], -1.0, dh[:], ALU.mult, ALU.mult)
+
+        def turn_da(e, halves=range(2)):
+            for h in halves:
+                turn(da_in[e][2 * h:2 * h + 2], da_turned[e][:, h * 1024:(h + 1) * 1024], (e, h) in (), da_banks[e][h])
+
+        def quantise_da(e):
+            da_mx[e] = quantise(da_turned[e][:], "da", 3)
+
+        def tokens(e):
+            for h in range(2):
+                for b in range(2 * h, 2 * h + 2):
+                    gather((b, e) in (), x_in[e][b][:], x_sb[b], e)
+
+        def turn_tokens(e, halves=range(2)):
+            for h in halves:
+                x_turned[e, h] = ring.tile([P, 2 * P * PACK], BF16, name="x_turned", align_bytes=64, bufs=4)
+                turn(x_in[e][2 * h:2 * h + 2], x_turned[e, h][:], (e, h) in (), x_banks[e][h])
+
+        def quantise_x(e, halves=range(2)):
+            for h in halves:
+                x_mx[e, h] = quantise(x_turned[e, h][:], "x", 6)
+
+        def weight_gradient(e, blocks=range(BLOCKS)):
+            for b in blocks:
+                x_codes, x_scales = x_mx[e, b // 2]
+                acc = banks[out_banks[e][b]]
+                cols = slice(b % 2 * P, (b % 2 + 1) * P)
+                nc.tensor.matmul_mx(out=acc[:], lhsT=x_codes[:, cols].bitcast(FP8X4), lhsT_scale=x_scales[:, cols],
+                                    rhs=da_mx[e][0][:].bitcast(FP8X4), rhs_scale=da_mx[e][1][:], start=True, stop=True)
+                result = ring.tile([P, H], F32, name="result", bufs=6)
+                psum_copy((e, b) in ((1,0),(1,1),(1,2),(1,3),(2,1),(2,3)), result[:], acc[:])
+                nc.sync.dma_start(out[e, b * P:(b + 1) * P, :], result[:])
+
+        sigmoid(0)
+        silu_slope(0)
+        sigmoid(1)
+        gather_dy(0)
+        gather_dy(1)
+        silu_slope(1)
+        gate_rows(0)
+        cast_w(0)
+        quantise_g(0)
+        quantise_w(0)
+        tokens(0)
+        tokens(1)
+        gate_rows(1)
+        turn_tokens(0, [0])
+        turn_tokens(1, [0])
+        hidden_gradient(0)
+        turn_da(0)
+        turn_tokens(0, [1])
+        turn_tokens(1, [1])
+        cast_w(1)
+        quantise_g(1)
+        quantise_w(1)
+        cast_w(2)
+        hidden_gradient(1)
+        sigmoid(2)
+        turn_da(1)
+        gather_dy(2)
+        quantise_w(2)
+        quantise_da(0)
+        quantise_x(0)
+        weight_gradient(0)
+        silu_slope(2)
+        quantise_x(1)
+        quantise_da(1)
+        gate_rows(2)
+        quantise_g(2)
+        weight_gradient(1)
+        hidden_gradient(2)
+        tokens(2)
+        turn_tokens(2, [0])
+        turn_da(2)
+        turn_tokens(2, [1])
+        quantise_x(2, [0])
+        quantise_da(2)
+        weight_gradient(2, [0, 1])
+        quantise_x(2, [1])
+        weight_gradient(2, [2, 3])

@@ -30,18 +30,20 @@ def tile_moe_mlp_silu_kernel(tc, xT, dyT, a, w2, gate, offs, out):
         psum = ctx.enter_context(tc.psum_pool(name="psum", bufs=2))
 
         offsets = keep.tile([P, E * OFFS_COLS], U16, name="offsets")
-        nc.sync.dma_start(offsets[:], offs)
 
         dy_rows = dyT.rearrange("(p j) t -> p j t", j=PACK)
         dy_sb = [keep.tile([P, T], F32, name=f"dy{j}") for j in range(PACK)]
         x_sb = [keep.tile([P, T], F32, name=f"x{b}") for b in range(BLOCKS)]
-        a_sb = [[keep.tile([P, 2, C], F32, name=f"a{e}_{h}") for h in range(2)] for e in range(E)]
+        a_parts = [[1, 1, 2], [2, 2], [2, 2]]
+        a_sb = [[keep.tile([P, n, C], F32, name=f"a{e}_{h}") for h, n in enumerate(a_parts[e])] for e in range(E)]
+        a_rows = [[a_sb[e][h][:, r, :] for h, n in enumerate(a_parts[e]) for r in range(n)] for e in range(E)]
+        a_first = [[sum(a_parts[e][:h]) for h in range(len(a_parts[e]))] for e in range(E)]
         gate_sb = [keep.tile([P, C], F32, name=f"gate{e}") for e in range(E)]
         w_sb = [keep.tile([P, PACK, H], F32, name=f"w{e}") for e in range(E)]
 
         def load_a(e):
-            for h in range(2):
-                rows = a[h * 2 * P:(h + 1) * 2 * P, e * C:(e + 1) * C]
+            for h, n in enumerate(a_parts[e]):
+                rows = a[a_first[e][h] * P:(a_first[e][h] + n) * P, e * C:(e + 1) * C]
                 nc.sync.dma_start(a_sb[e][h][:], rows.rearrange("(b p) s -> p b s", p=P))
 
         def load_w(e):
@@ -57,38 +59,39 @@ def tile_moe_mlp_silu_kernel(tc, xT, dyT, a, w2, gate, offs, out):
             nc.sync.dma_start(x_sb[b][:], xT[b * P:(b + 1) * P, :])
 
         load_a(0)
+        nc.sync.dma_start(offsets[:], offs)
+        load_a(1)
         load_dy(0)
         load_dy(1)
-        load_a(1)
         load_dy(2)
         load_dy(3)
         load_gate(0)
+        load_x(0)
         load_w(0)
         load_gate(1)
-        load_x(0)
         load_x(1)
         load_w(1)
         load_x(2)
+        load_gate(2)
+        load_a(2)
         load_x(3)
         load_w(2)
-        load_a(2)
-        load_gate(2)
 
         ident = keep.tile([P, P], F32, name="ident")
         make_identity(nc, ident[:])
 
         work = [keep.tile([P, PACK * C], F32, name=f"work{n}") for n in range(3)]
         sig_in = [work[0], work[2], work[2]]
-        dy_in = [work[1][:], work[0][:], w_sb[1][:].rearrange("p j i -> p (j i)")]
+        dy_in = [work[1], work[0], work[1]]
         rows_bf = [[keep.tile([P, C], BF16, name=f"rows{n}_{b}") for b in range(BLOCKS)] for n in range(3)]
         da_in = [rows_bf[2], rows_bf[2], rows_bf[0]]
         x_in = [rows_bf[0], rows_bf[1], rows_bf[2]]
 
         banks = [psum.tile([P, C], F32, name=f"bank{n}", bufs=1) for n in range(8)]
-        dh_banks = [(0, 1, 2, 3), (2, 3, 4, 5), (4, 5, 6, 7)]
-        da_banks = [(6, 7), (6, 7), (5, 6)]
-        x_banks = [(4, 0), (5, 1), (4, 7)]
-        out_banks = [(0, 1, 2, 3), (0, 1, 2, 3), (0, 1, 2, 3)]
+        dh_banks = [(0, 1, 2, 3), (2, 3, 4, 5), (2, 6, 7, 3)]
+        da_banks = [(6, 7), (6, 7), (2, 7)]
+        x_banks = [(0, 2), (1, 3), (6, 3)]
+        out_banks = [(4, 5, 0, 1), (4, 5, 0, 1), (4, 5, 0, 1)]
 
         def gather(on_vector, dst, window, e):
             picked = window[:].indirect(offsets[:, e * OFFS_COLS:(e + 1) * OFFS_COLS])
@@ -120,25 +123,27 @@ def tile_moe_mlp_silu_kernel(tc, xT, dyT, a, w2, gate, offs, out):
                       bank.rearrange("p b u c -> p b c u"))
 
         def sigmoid(e):
-            for h in range(2):
-                nc.scalar.activation(sig_in[e][:, h * 2 * C:(h + 1) * 2 * C],
+            for h, n in enumerate(a_parts[e]):
+                nc.scalar.activation(sig_in[e][:, a_first[e][h] * C:(a_first[e][h] + n) * C],
                                      a_sb[e][h][:].rearrange("p b s -> p (b s)"), ACT.Sigmoid)
 
-        def silu_slope(e):
-            for step in range(2):
-                for h in range(2):
-                    v = a_sb[e][h][:].rearrange("p b s -> p (b s)")
-                    sig = sig_in[e][:, h * 2 * C:(h + 1) * 2 * C]
-                    if step == 0:
-                        nc.vector.scalar_tensor_tensor(v, sig, 1.0, v, ALU.subtract, ALU.mult)
-                    else:
-                        nc.vector.scalar_tensor_tensor(v, v, 1.0, sig, ALU.subtract, ALU.mult)
+        def silu_slope(e, steps=None):
+            last = len(a_parts[e])
+            for step in steps or range(last + 1):
+                for h, stage in ((step, 0), (step - 1, 1)):
+                    if 0 <= h < last:
+                        v = a_sb[e][h][:].rearrange("p b s -> p (b s)")
+                        sig = sig_in[e][:, a_first[e][h] * C:(a_first[e][h] + a_parts[e][h]) * C]
+                        if stage == 0:
+                            nc.vector.scalar_tensor_tensor(v, sig, 1.0, v, ALU.subtract, ALU.mult)
+                        else:
+                            nc.vector.scalar_tensor_tensor(v, v, 1.0, sig, ALU.subtract, ALU.mult)
 
         g_mx, w_mx, da_mx, x_mx, g_bf, w_bf, da_turned, x_turned = {}, {}, {}, {}, {}, {}, {}, {}
 
         def gather_dy(e):
             for j in range(PACK):
-                gather((j, e) in ((0, 1),), dy_in[e][:, j * C:(j + 1) * C], dy_sb[j], e)
+                gather((j, e) in ((1, 1), (2, 1)), dy_in[e][:, j * C:(j + 1) * C], dy_sb[j], e)
 
         def gate_rows(e):
             g_bf[e] = ring.tile([P, C * PACK], BF16, name="g_bf", align_bytes=64)
@@ -166,14 +171,29 @@ def tile_moe_mlp_silu_kernel(tc, xT, dyT, a, w2, gate, offs, out):
                     cols = slice(b * P, (b + 1) * P)
                     nc.tensor.matmul_mx(out=dh[:], lhsT=w_mx[e][0][:, cols].bitcast(FP8X4), lhsT_scale=w_mx[e][1][:, cols],
                                         rhs=g_mx[e][0][:].bitcast(FP8X4), rhs_scale=g_mx[e][1][:], start=True, stop=True)
-                    nc.vector.scalar_tensor_tensor(da_in[e][b][:], a_sb[e][h][:, b % 2, :], -1.0, dh[:], ALU.mult, ALU.mult)
+                    nc.vector.scalar_tensor_tensor(da_in[e][b][:], a_rows[e][b], -1.0, dh[:], ALU.mult, ALU.mult)
 
         def turn_da(e, halves=range(2)):
             for h in halves:
-                turn(da_in[e][2 * h:2 * h + 2], da_turned[e][:, h * 1024:(h + 1) * 1024], (e, h) in (), da_banks[e][h])
+                turn(da_in[e][2 * h:2 * h + 2], da_turned[e][:, h * 1024:(h + 1) * 1024], (e, h) in ((2,0),(2,1)), da_banks[e][h])
 
         def quantise_da(e):
             da_mx[e] = quantise(da_turned[e][:], "da", 3)
+
+        def quantise_da_half(e, h):
+            da_mx[e, h] = quantise(da_turned[e][:, h * 1024:(h + 1) * 1024], "dah", 2)
+
+        def quarter(e, g, h, n, on_vector):
+            x_codes, x_scales = x_mx[e, g]
+            acc = banks[n]
+            for b in range(2):
+                cols = slice(b * P, (b + 1) * P)
+                nc.tensor.matmul_mx(out=acc[:, b * 256:(b + 1) * 256], lhsT=x_codes[:, cols].bitcast(FP8X4), lhsT_scale=x_scales[:, cols],
+                                    rhs=da_mx[e, h][0][:].bitcast(FP8X4), rhs_scale=da_mx[e, h][1][:], start=True, stop=True)
+            result = ring.tile([P, H], F32, name="result", bufs=8)
+            psum_copy(on_vector, result[:], acc[:])
+            nc.sync.dma_start(out[e, 2 * g * P:(2 * g + 2) * P, h * 256:(h + 1) * 256].rearrange("(b p) i -> p b i", p=P),
+                              result[:].rearrange("p (b i) -> p b i", b=2))
 
         def tokens(e):
             for h in range(2):
@@ -182,7 +202,7 @@ def tile_moe_mlp_silu_kernel(tc, xT, dyT, a, w2, gate, offs, out):
 
         def turn_tokens(e, halves=range(2)):
             for h in halves:
-                x_turned[e, h] = ring.tile([P, 2 * P * PACK], BF16, name="x_turned", align_bytes=64, bufs=4)
+                x_turned[e, h] = ring.tile([P, 2 * P * PACK], BF16, name="x_turned", align_bytes=64, bufs=6)
                 turn(x_in[e][2 * h:2 * h + 2], x_turned[e, h][:], (e, h) in (), x_banks[e][h])
 
         def quantise_x(e, halves=range(2)):
@@ -196,54 +216,56 @@ def tile_moe_mlp_silu_kernel(tc, xT, dyT, a, w2, gate, offs, out):
                 cols = slice(b % 2 * P, (b % 2 + 1) * P)
                 nc.tensor.matmul_mx(out=acc[:], lhsT=x_codes[:, cols].bitcast(FP8X4), lhsT_scale=x_scales[:, cols],
                                     rhs=da_mx[e][0][:].bitcast(FP8X4), rhs_scale=da_mx[e][1][:], start=True, stop=True)
-                result = ring.tile([P, H], F32, name="result", bufs=6)
-                psum_copy((e, b) in ((1,0),(1,1),(1,2),(1,3),(2,1),(2,3)), result[:], acc[:])
+                result = ring.tile([P, H], F32, name="result", bufs=8)
+                psum_copy((e, b) in ((1,0),(1,1),(2,1),(2,3)), result[:], acc[:])
                 nc.sync.dma_start(out[e, b * P:(b + 1) * P, :], result[:])
 
         sigmoid(0)
         silu_slope(0)
         sigmoid(1)
+        silu_slope(1)
         gather_dy(0)
         gather_dy(1)
-        silu_slope(1)
         gate_rows(0)
         cast_w(0)
         quantise_g(0)
         quantise_w(0)
         tokens(0)
         tokens(1)
+        gather_dy(2)
         gate_rows(1)
-        turn_tokens(0, [0])
-        turn_tokens(1, [0])
         hidden_gradient(0)
         turn_da(0)
-        turn_tokens(0, [1])
-        turn_tokens(1, [1])
+        turn_tokens(0, [0])
+        turn_tokens(1, [0])
         cast_w(1)
         quantise_g(1)
         quantise_w(1)
-        cast_w(2)
         hidden_gradient(1)
         sigmoid(2)
+        turn_tokens(0, [1])
         turn_da(1)
-        gather_dy(2)
+        turn_tokens(1, [1])
+        gate_rows(2)
+        cast_w(2)
+        quantise_g(2)
         quantise_w(2)
         quantise_da(0)
+        silu_slope(2, [0, 1])
         quantise_x(0)
         weight_gradient(0)
-        silu_slope(2)
+        x_in[2] = rows_bf[2][:2] + [x_turned[0, 1][:, b * C:(b + 1) * C] for b in range(2)]
+        silu_slope(2, [2])
         quantise_x(1)
         quantise_da(1)
-        gate_rows(2)
-        quantise_g(2)
-        weight_gradient(1)
         hidden_gradient(2)
         tokens(2)
+        weight_gradient(1)
+        turn_da(2, [0])
         turn_tokens(2, [0])
-        turn_da(2)
+        turn_da(2, [1])
         turn_tokens(2, [1])
         quantise_x(2, [0])
         quantise_da(2)
-        weight_gradient(2, [0, 1])
         quantise_x(2, [1])
-        weight_gradient(2, [2, 3])
+        weight_gradient(2)

@@ -73,9 +73,9 @@ def tile_moe_mlp_silu_kernel(tc, xT, dyT, a, w2, gate, offs, out):
         load_w(1)
         load_x(2)
         load_gate(2)
+        load_w(2)
         load_a(2)
         load_x(3)
-        load_w(2)
 
         ident = keep.tile([P, P], F32, name="ident")
         make_identity(nc, ident[:])
@@ -88,10 +88,10 @@ def tile_moe_mlp_silu_kernel(tc, xT, dyT, a, w2, gate, offs, out):
         x_in = [rows_bf[0], rows_bf[1], rows_bf[2]]
 
         banks = [psum.tile([P, C], F32, name=f"bank{n}", bufs=1) for n in range(8)]
-        dh_banks = [(0, 1, 2, 3), (2, 3, 4, 5), (2, 6, 7, 3)]
-        da_banks = [(6, 7), (6, 7), (2, 7)]
-        x_banks = [(0, 2), (1, 3), (6, 3)]
-        out_banks = [(4, 5, 0, 1), (4, 5, 0, 1), (4, 5, 0, 1)]
+        dh_banks = [(0, 1, 2, 3), (2, 3, 4, 5), (2, 3, 4, 5)]
+        da_banks = [(6, 7), (6, 7), (2, 4)]
+        x_banks = [(0, 6), (1, 7), (6, 3)]
+        out_banks = [(0, 1, 6, 7), (0, 1, 2, 5), ()]
 
         def gather(on_vector, dst, window, e):
             picked = window[:].indirect(offsets[:, e * OFFS_COLS:(e + 1) * OFFS_COLS])
@@ -139,7 +139,8 @@ def tile_moe_mlp_silu_kernel(tc, xT, dyT, a, w2, gate, offs, out):
                         else:
                             nc.vector.scalar_tensor_tensor(v, v, 1.0, sig, ALU.subtract, ALU.mult)
 
-        g_mx, w_mx, da_mx, x_mx, g_bf, w_bf, da_turned, x_turned = {}, {}, {}, {}, {}, {}, {}, {}
+        g_mx, w_mx, da_mx, x_mx, g_bf, da_turned, x_turned = {}, {}, {}, {}, {}, {}, {}
+        w_bf = keep.tile([P, H * PACK], BF16, name="w_bf", align_bytes=64)
 
         def gather_dy(e):
             for j in range(PACK):
@@ -153,15 +154,19 @@ def tile_moe_mlp_silu_kernel(tc, xT, dyT, a, w2, gate, offs, out):
                                     gate_e.unsqueeze(2).to_broadcast([P, C // 2, PACK, 2]), ALU.mult)
 
         def cast_w(e):
-            w_bf[e] = ring.tile([P, H * PACK], BF16, name="w_bf", align_bytes=64)
-            nc.vector.tensor_copy(w_bf[e][:].rearrange("p (c i j) -> p c j i", i=2, j=PACK),
-                                  w_sb[e][:].rearrange("p j (c i) -> p c j i", i=2))
+            dst = w_bf[:].rearrange("p (c i j) -> p c j i", i=2, j=PACK)
+            src = w_sb[e][:].rearrange("p j (c i) -> p c j i", i=2)
+            if e in (1, 2):
+                nc.gpsimd.tensor_scalar(w_bf[:].rearrange("p (i j) -> p i j", j=PACK), w_sb[e][:].rearrange("p j i -> p i j"),
+                                        1.0, 0.0, ALU.mult, ALU.add)
+            else:
+                nc.vector.tensor_copy(dst, src)
 
         def quantise_g(e):
             g_mx[e] = quantise(g_bf[e][:], "g", 2)
 
         def quantise_w(e):
-            w_mx[e] = quantise(w_bf[e][:], "w", 3)
+            w_mx[e] = quantise(w_bf[:], "w", 3)
 
         def hidden_gradient(e):
             da_turned[e] = ring.tile([P, H * PACK], BF16, name="da_turned", align_bytes=64)
@@ -175,7 +180,7 @@ def tile_moe_mlp_silu_kernel(tc, xT, dyT, a, w2, gate, offs, out):
 
         def turn_da(e, halves=range(2)):
             for h in halves:
-                turn(da_in[e][2 * h:2 * h + 2], da_turned[e][:, h * 1024:(h + 1) * 1024], (e, h) in ((2,0),(2,1)), da_banks[e][h])
+                turn(da_in[e][2 * h:2 * h + 2], da_turned[e][:, h * 1024:(h + 1) * 1024], (e, h) in ((0,0),(1,0),(1,1),(2,0),(2,1)), da_banks[e][h])
 
         def quantise_da(e):
             da_mx[e] = quantise(da_turned[e][:], "da", 3)
@@ -217,7 +222,7 @@ def tile_moe_mlp_silu_kernel(tc, xT, dyT, a, w2, gate, offs, out):
                 nc.tensor.matmul_mx(out=acc[:], lhsT=x_codes[:, cols].bitcast(FP8X4), lhsT_scale=x_scales[:, cols],
                                     rhs=da_mx[e][0][:].bitcast(FP8X4), rhs_scale=da_mx[e][1][:], start=True, stop=True)
                 result = ring.tile([P, H], F32, name="result", bufs=8)
-                psum_copy((e, b) in ((1,0),(1,1),(2,1),(2,3)), result[:], acc[:])
+                psum_copy((e, b) in ((0,2),), result[:], acc[:])
                 nc.sync.dma_start(out[e, b * P:(b + 1) * P, :], result[:])
 
         sigmoid(0)
@@ -229,43 +234,50 @@ def tile_moe_mlp_silu_kernel(tc, xT, dyT, a, w2, gate, offs, out):
         gate_rows(0)
         cast_w(0)
         quantise_g(0)
-        quantise_w(0)
         tokens(0)
         tokens(1)
         gather_dy(2)
         gate_rows(1)
+        quantise_w(0)
+        quantise_g(1)
+        cast_w(1)
         hidden_gradient(0)
         turn_da(0)
         turn_tokens(0, [0])
         turn_tokens(1, [0])
-        cast_w(1)
-        quantise_g(1)
         quantise_w(1)
-        hidden_gradient(1)
-        sigmoid(2)
-        turn_tokens(0, [1])
-        turn_da(1)
-        turn_tokens(1, [1])
         gate_rows(2)
         cast_w(2)
+        hidden_gradient(1)
+        sigmoid(2)
+        turn_da(1)
+        turn_tokens(0, [1])
+        turn_tokens(1, [1])
         quantise_g(2)
         quantise_w(2)
         quantise_da(0)
+        quantise_x(0, [0])
+        weight_gradient(0, [0, 1])
         silu_slope(2, [0, 1])
-        quantise_x(0)
-        weight_gradient(0)
-        x_in[2] = rows_bf[2][:2] + [x_turned[0, 1][:, b * C:(b + 1) * C] for b in range(2)]
+        quantise_x(0, [1])
+        x_in[2] = [x_turned[0, b // 2][:, b % 2 * C:(b % 2 + 1) * C] for b in range(BLOCKS)]
+        tokens(2)
+        weight_gradient(0, [2, 3])
         silu_slope(2, [2])
         quantise_x(1)
         quantise_da(1)
         hidden_gradient(2)
-        tokens(2)
-        weight_gradient(1)
-        turn_da(2, [0])
         turn_tokens(2, [0])
-        turn_da(2, [1])
+        weight_gradient(1, [0, 1])
+        turn_da(2, [0])
         turn_tokens(2, [1])
+        turn_da(2, [1])
         quantise_x(2, [0])
-        quantise_da(2)
+        quantise_da_half(2, 0)
+        quantise_da_half(2, 1)
         quantise_x(2, [1])
-        weight_gradient(2)
+        weight_gradient(1, [2, 3])
+        quarter(2, 0, 0, 6, False)
+        quarter(2, 0, 1, 7, True)
+        quarter(2, 1, 0, 0, False)
+        quarter(2, 1, 1, 1, True)

@@ -34,17 +34,17 @@ def tile_moe_mlp_silu_kernel(tc, xT, dyT, a, w2, gate, offs, out):
         dy_rows = dyT.rearrange("(p j) t -> p j t", j=PACK)
         dy_sb = [keep.tile([P, T], F32, name=f"dy{j}") for j in range(PACK)]
         x_sb = [keep.tile([P, T], F32, name=f"x{b}") for b in range(BLOCKS)]
-        a_parts = [[1, 1, 2], [2, 2], [2, 2]]
-        a_sb = [[keep.tile([P, n, C], F32, name=f"a{e}_{h}") for h, n in enumerate(a_parts[e])] for e in range(E)]
-        a_rows = [[a_sb[e][h][:, r, :] for h, n in enumerate(a_parts[e]) for r in range(n)] for e in range(E)]
-        a_first = [[sum(a_parts[e][:h]) for h in range(len(a_parts[e]))] for e in range(E)]
+        a_parts = [[(0, 1, 0, 256), (0, 1, 256, 256), (1, 1, 0, C), (2, 2, 0, C)]] + [[(0, 2, 0, C), (2, 2, 0, C)]] * 2
+        a_sb = [keep.tile([P, BLOCKS * C], F32, name=f"a{e}") for e in range(E)]
+        a_rows = [[a_sb[e][:, b * C:(b + 1) * C] for b in range(BLOCKS)] for e in range(E)]
+        a_cols = [[slice(b * C + s, (b + n - 1) * C + s + w) for b, n, s, w in a_parts[e]] for e in range(E)]
         gate_sb = [keep.tile([P, C], F32, name=f"gate{e}") for e in range(E)]
         w_sb = [keep.tile([P, PACK, H], F32, name=f"w{e}") for e in range(E)]
 
         def load_a(e):
-            for h, n in enumerate(a_parts[e]):
-                rows = a[a_first[e][h] * P:(a_first[e][h] + n) * P, e * C:(e + 1) * C]
-                nc.sync.dma_start(a_sb[e][h][:], rows.rearrange("(b p) s -> p b s", p=P))
+            for h, (b, n, s, w) in enumerate(a_parts[e]):
+                rows = a[b * P:(b + n) * P, e * C + s:e * C + s + w]
+                nc.sync.dma_start(a_sb[e][:, a_cols[e][h]].rearrange("p (b s) -> p b s", b=n), rows.rearrange("(b p) s -> p b s", p=P))
 
         def load_w(e):
             nc.sync.dma_start(w_sb[e][:], w2[e].rearrange("(p j) i -> p j i", j=PACK))
@@ -123,17 +123,16 @@ def tile_moe_mlp_silu_kernel(tc, xT, dyT, a, w2, gate, offs, out):
                       bank.rearrange("p b u c -> p b c u"))
 
         def sigmoid(e):
-            for h, n in enumerate(a_parts[e]):
-                nc.scalar.activation(sig_in[e][:, a_first[e][h] * C:(a_first[e][h] + n) * C],
-                                     a_sb[e][h][:].rearrange("p b s -> p (b s)"), ACT.Sigmoid)
+            for cols in a_cols[e]:
+                nc.scalar.activation(sig_in[e][:, cols], a_sb[e][:, cols], ACT.Sigmoid)
 
         def silu_slope(e, steps=None):
             last = len(a_parts[e])
             for step in steps or range(last + 1):
                 for h, stage in ((step, 0), (step - 1, 1)):
                     if 0 <= h < last:
-                        v = a_sb[e][h][:].rearrange("p b s -> p (b s)")
-                        sig = sig_in[e][:, a_first[e][h] * C:(a_first[e][h] + a_parts[e][h]) * C]
+                        v = a_sb[e][:, a_cols[e][h]]
+                        sig = sig_in[e][:, a_cols[e][h]]
                         if stage == 0:
                             nc.vector.scalar_tensor_tensor(v, sig, 1.0, v, ALU.subtract, ALU.mult)
                         else:
@@ -180,7 +179,7 @@ def tile_moe_mlp_silu_kernel(tc, xT, dyT, a, w2, gate, offs, out):
 
         def turn_da(e, halves=range(2)):
             for h in halves:
-                turn(da_in[e][2 * h:2 * h + 2], da_turned[e][:, h * 1024:(h + 1) * 1024], (e, h) in ((0,0),(1,0),(1,1),(2,0),(2,1)), da_banks[e][h])
+                turn(da_in[e][2 * h:2 * h + 2], da_turned[e][:, h * 1024:(h + 1) * 1024], (e, h) in ((1,0),(1,1),(2,0),(2,1)), da_banks[e][h])
 
         def quantise_da(e):
             da_mx[e] = quantise(da_turned[e][:], "da", 3)

from contextlib import ExitStack

import concourse.mybir as mybir
from concourse.masks import make_identity

K, T, E, C, H, N = 512, 1536, 3, 512, 512, 512
FLOPS = 2 * E * C * (N * H + K * H)
BYTES = 4 * (K * T + N * T + H * E * C + E * N * H + E * C + E * K * H) + 2 * 128 * 96

F32 = mybir.dt.float32
BF16 = mybir.dt.bfloat16
U32 = mybir.dt.uint32
U16 = mybir.dt.uint16
U8 = mybir.dt.uint8
FP8X4 = mybir.dt.float8_e4m3fn_x4
ALU = mybir.AluOpType
ACT = mybir.ActivationFunctionType

P = 128
PACK = 4
BLOCKS = 4
OFFS_COLS = C // 16


def tile_moe_mlp_silu_kernel(tc, xT, dyT, a, w2, gate, offs, out):
    nc = tc.nc
    with ExitStack() as ctx:
        keep = ctx.enter_context(tc.tile_pool(name="keep", bufs=1))
        ring = ctx.enter_context(tc.tile_pool(name="ring", bufs=2))
        psum = ctx.enter_context(tc.psum_pool(name="psum", bufs=2))

        offsets = keep.tile([P, E * OFFS_COLS], U16, name="offsets")

        dy_rows = dyT.rearrange("(p j) t -> p j t", j=PACK)
        dy_sb = [keep.tile([P, T], F32, name=f"dy{j}") for j in range(PACK)]
        x_sb = [keep.tile([P, T], F32, name=f"x{b}") for b in range(BLOCKS)]
        a_parts = [[(0, 1, 0, 256), (0, 1, 256, 256), (1, 1, 0, C), (2, 2, 0, C)]] + [[(0, 2, 0, C), (2, 2, 0, C)]] * 2
        a_sb = [keep.tile([P, BLOCKS * C], F32, name=f"a{e}") for e in range(E)]
        a_rows = [[a_sb[e][:, b * C:(b + 1) * C] for b in range(BLOCKS)] for e in range(E)]
        a_cols = [[slice(b * C + s, (b + n - 1) * C + s + w) for b, n, s, w in a_parts[e]] for e in range(E)]
        gate_sb = [keep.tile([P, C], F32, name=f"gate{e}") for e in range(E)]
        w_sb = [keep.tile([P, PACK, H], F32, name=f"w{e}") for e in range(E)]

        def load_a(e):
            for h, (b, n, s, w) in enumerate(a_parts[e]):
                rows = a[b * P:(b + n) * P, e * C + s:e * C + s + w]
                nc.sync.dma_start(a_sb[e][:, a_cols[e][h]].rearrange("p (b s) -> p b s", b=n), rows.rearrange("(b p) s -> p b s", p=P))

        def load_w(e):
            nc.sync.dma_start(w_sb[e][:], w2[e].rearrange("(p j) i -> p j i", j=PACK))

        def load_gate(e):
            nc.sync.dma_start(gate_sb[e][:], gate[0:P, e * C:(e + 1) * C])

        def load_dy(j):
            nc.sync.dma_start(dy_sb[j][:], dy_rows[:, j, :])

        def load_x(b):
            nc.sync.dma_start(x_sb[b][:], xT[b * P:(b + 1) * P, :])

        load_a(0)
        nc.sync.dma_start(offsets[:], offs)
        load_a(1)
        load_dy(0)
        load_dy(1)
        load_dy(2)
        load_dy(3)
        load_gate(0)
        load_x(0)
        load_w(0)
        load_gate(1)
        load_x(1)
        load_w(1)
        load_x(2)
        load_gate(2)
        load_w(2)
        load_a(2)
        load_x(3)

        ident = keep.tile([P, P], F32, name="ident")
        make_identity(nc, ident[:])

        work = [keep.tile([P, PACK * C], F32, name=f"work{n}") for n in range(3)]
        sig_in = [work[0], work[2], work[2]]
        dy_in = [work[1], work[0], work[1]]
        rows_bf = [[keep.tile([P, C], BF16, name=f"rows{n}_{b}") for b in range(BLOCKS)] for n in range(3)]
        da_in = [rows_bf[2], rows_bf[2], rows_bf[0]]
        x_in = [rows_bf[0], rows_bf[1], rows_bf[2]]

        banks = [psum.tile([P, C], F32, name=f"bank{n}", bufs=1) for n in range(8)]
        dh_banks = [(0, 1, 2, 3), (2, 3, 4, 5), (2, 3, 4, 5)]
        da_banks = [(6, 7), (6, 7), (2, 4)]
        x_banks = [(0, 6), (1, 7), (6, 3)]
        out_banks = [(0, 1, 6, 7), (0, 1, 2, 5), ()]

        def gather(on_vector, dst, window, e):
            picked = window[:].indirect(offsets[:, e * OFFS_COLS:(e + 1) * OFFS_COLS])
            if on_vector:
                nc.vector.tensor_copy(dst, picked)
            else:
                nc.scalar.activation(dst, picked, ACT.Copy)

        def quantise(values, name, bufs):
            width = values.shape[1] // PACK
            codes = ring.tile([P, width], U32, name=name + "_codes", align_bytes=64, bufs=bufs)
            scales = ring.tile([P, width], U8, name=name + "_scales", align_bytes=64, bufs=bufs)
            nc.vector.quantize_mx(out=codes[:].bitcast(FP8X4), scales=scales[:], in_=values)
            return codes, scales

        def psum_copy(on_vector, dst, src):
            if on_vector:
                nc.vector.tensor_copy(dst, src)
            else:
                nc.scalar.copy(dst, src)

        def turn(pair, dst, on_vector, n):
            bank = banks[n][:].rearrange("p (b u c) -> p b u c", b=2, u=2)
            for b in range(2):
                words = pair[b][:].bitcast(F32)
                for u in range(2):
                    nc.tensor.transpose(bank[:, b, u, :], words[:, u::2], ident[:])
            psum_copy(on_vector, dst.bitcast(F32).rearrange("p (b c u) -> p b c u", b=2, u=2),
                      bank.rearrange("p b u c -> p b c u"))

        def sigmoid(e):
            for cols in a_cols[e]:
                nc.scalar.activation(sig_in[e][:, cols], a_sb[e][:, cols], ACT.Sigmoid)

        def silu_slope(e, steps=None):
            last = len(a_parts[e])
            for step in steps or range(last + 1):
                for h, stage in ((step, 0), (step - 1, 1)):
                    if 0 <= h < last:
                        v = a_sb[e][:, a_cols[e][h]]
                        sig = sig_in[e][:, a_cols[e][h]]
                        if stage == 0:
                            nc.vector.scalar_tensor_tensor(v, sig, 1.0, v, ALU.subtract, ALU.mult)
                        else:
                            nc.vector.scalar_tensor_tensor(v, v, 1.0, sig, ALU.subtract, ALU.mult)

        g_mx, w_mx, da_mx, x_mx, g_bf, da_turned, x_turned = {}, {}, {}, {}, {}, {}, {}
        w_bf = keep.tile([P, H * PACK], BF16, name="w_bf", align_bytes=64)

        def gather_dy(e):
            for j in range(PACK):
                gather((j, e) in ((1, 1), (2, 1)), dy_in[e][:, j * C:(j + 1) * C], dy_sb[j], e)

        def gate_rows(e):
            g_bf[e] = ring.tile([P, C * PACK], BF16, name="g_bf", align_bytes=64)
            gate_e = gate_sb[e][:].rearrange("p (c i) -> p c i", i=2)
            nc.vector.tensor_tensor(g_bf[e][:].rearrange("p (c i j) -> p c j i", i=2, j=PACK),
                                    dy_in[e][:].rearrange("p (j c i) -> p c j i", j=PACK, i=2),
                                    gate_e.unsqueeze(2).to_broadcast([P, C // 2, PACK, 2]), ALU.mult)

        def cast_w(e):
            dst = w_bf[:].rearrange("p (c i j) -> p c j i", i=2, j=PACK)
            src = w_sb[e][:].rearrange("p j (c i) -> p c j i", i=2)
            if e in (1, 2):
                nc.gpsimd.tensor_scalar(w_bf[:].rearrange("p (i j) -> p i j", j=PACK), w_sb[e][:].rearrange("p j i -> p i j"),
                                        1.0, 0.0, ALU.mult, ALU.add)
            else:
                nc.vector.tensor_copy(dst, src)

        def quantise_g(e):
            g_mx[e] = quantise(g_bf[e][:], "g", 2)

        def quantise_w(e):
            w_mx[e] = quantise(w_bf[:], "w", 3)

        def hidden_gradient(e):
            da_turned[e] = ring.tile([P, H * PACK], BF16, name="da_turned", align_bytes=64)
            for h in range(2):
                for b in range(2 * h, 2 * h + 2):
                    dh = banks[dh_banks[e][b]]
                    cols = slice(b * P, (b + 1) * P)
                    nc.tensor.matmul_mx(out=dh[:], lhsT=w_mx[e][0][:, cols].bitcast(FP8X4), lhsT_scale=w_mx[e][1][:, cols],
                                        rhs=g_mx[e][0][:].bitcast(FP8X4), rhs_scale=g_mx[e][1][:], start=True, stop=True)
                    nc.vector.scalar_tensor_tensor(da_in[e][b][:], a_rows[e][b], -1.0, dh[:], ALU.mult, ALU.mult)

        def turn_da(e, halves=range(2)):
            for h in halves:
                turn(da_in[e][2 * h:2 * h + 2], da_turned[e][:, h * 1024:(h + 1) * 1024], (e, h) in ((1,0),(1,1),(2,0),(2,1)), da_banks[e][h])

        def quantise_da(e):
            da_mx[e] = quantise(da_turned[e][:], "da", 3)

        def quantise_da_half(e, h):
            da_mx[e, h] = quantise(da_turned[e][:, h * 1024:(h + 1) * 1024], "dah", 2)

        def quarter(e, g, h, n, on_vector):
            x_codes, x_scales = x_mx[e, g]
            acc = banks[n]
            for b in range(2):
                cols = slice(b * P, (b + 1) * P)
                nc.tensor.matmul_mx(out=acc[:, b * 256:(b + 1) * 256], lhsT=x_codes[:, cols].bitcast(FP8X4), lhsT_scale=x_scales[:, cols],
                                    rhs=da_mx[e, h][0][:].bitcast(FP8X4), rhs_scale=da_mx[e, h][1][:], start=True, stop=True)
            result = ring.tile([P, H], F32, name="result", bufs=8)
            psum_copy(on_vector, result[:], acc[:])
            nc.sync.dma_start(out[e, 2 * g * P:(2 * g + 2) * P, h * 256:(h + 1) * 256].rearrange("(b p) i -> p b i", p=P),
                              result[:].rearrange("p (b i) -> p b i", b=2))

        def tokens(e):
            for h in range(2):
                for b in range(2 * h, 2 * h + 2):
                    gather((b, e) in (), x_in[e][b][:], x_sb[b], e)

        def turn_tokens(e, halves=range(2)):
            for h in halves:
                x_turned[e, h] = ring.tile([P, 2 * P * PACK], BF16, name="x_turned", align_bytes=64, bufs=6)
                turn(x_in[e][2 * h:2 * h + 2], x_turned[e, h][:], (e, h) in (), x_banks[e][h])

        def quantise_x(e, halves=range(2)):
            for h in halves:
                x_mx[e, h] = quantise(x_turned[e, h][:], "x", 6)

        def weight_gradient(e, blocks=range(BLOCKS)):
            for b in blocks:
                x_codes, x_scales = x_mx[e, b // 2]
                acc = banks[out_banks[e][b]]
                cols = slice(b % 2 * P, (b % 2 + 1) * P)
                nc.tensor.matmul_mx(out=acc[:], lhsT=x_codes[:, cols].bitcast(FP8X4), lhsT_scale=x_scales[:, cols],
                                    rhs=da_mx[e][0][:].bitcast(FP8X4), rhs_scale=da_mx[e][1][:], start=True, stop=True)
                result = ring.tile([P, H], F32, name="result", bufs=8)
                psum_copy((e, b) in ((0,2),), result[:], acc[:])
                nc.sync.dma_start(out[e, b * P:(b + 1) * P, :], result[:])

        sigmoid(0)
        silu_slope(0)
        sigmoid(1)
        silu_slope(1)
        gather_dy(0)
        gather_dy(1)
        gate_rows(0)
        cast_w(0)
        quantise_g(0)
        tokens(0)
        tokens(1)
        gather_dy(2)
        gate_rows(1)
        quantise_w(0)
        quantise_g(1)
        cast_w(1)
        hidden_gradient(0)
        turn_da(0)
        turn_tokens(0, [0])
        turn_tokens(1, [0])
        quantise_w(1)
        gate_rows(2)
        cast_w(2)
        hidden_gradient(1)
        sigmoid(2)
        turn_da(1)
        turn_tokens(0, [1])
        turn_tokens(1, [1])
        quantise_g(2)
        quantise_w(2)
        quantise_da(0)
        quantise_x(0, [0])
        weight_gradient(0, [0, 1])
        silu_slope(2, [0, 1])
        quantise_x(0, [1])
        x_in[2] = [x_turned[0, b // 2][:, b % 2 * C:(b % 2 + 1) * C] for b in range(BLOCKS)]
        tokens(2)
        weight_gradient(0, [2, 3])
        silu_slope(2, [2])
        quantise_x(1)
        quantise_da(1)
        hidden_gradient(2)
        turn_tokens(2, [0])
        weight_gradient(1, [0, 1])
        turn_da(2, [0])
        turn_tokens(2, [1])
        turn_da(2, [1])
        quantise_x(2, [0])
        quantise_da_half(2, 0)
        quantise_da_half(2, 1)
        quantise_x(2, [1])
        weight_gradient(1, [2, 3])
        quarter(2, 0, 0, 6, False)
        quarter(2, 0, 1, 7, True)
        quarter(2, 1, 0, 0, False)
        quarter(2, 1, 1, 1, True)
